import numpy as np
import ml_dtypes


def mxq(x, axis, fmt="e4m3"):
    dtype, down = {"e4m3": (ml_dtypes.float8_e4m3fn, 7), "e5m2": (ml_dtypes.float8_e5m2, 14)}[fmt]
    v = np.moveaxis(np.asarray(x, np.float32).astype(ml_dtypes.bfloat16).astype(np.float64), axis, -1)
    blocks = v.reshape(v.shape[:-1] + (-1, 32))
    amax = np.abs(blocks).max(-1, keepdims=True)
    byte = np.maximum(np.where(amax > 0, np.frexp(amax)[1] - 1 + 127, 0) - down, 1)
    scale = np.exp2(byte - 127.0)
    codes = (blocks / scale).astype(np.float32).astype(dtype).astype(np.float64)
    return np.moveaxis((codes * scale).reshape(v.shape), -1, axis)


WIDE = False


def mx_kscale(k):
    if not WIDE:
        return np.ones(k)
    levels = np.array([10, -10, 5, -5, 0])
    if k % 512:
        return np.exp2(np.random.permutation(np.resize(levels, k // 32))).repeat(32)
    a = np.empty((k // 512, 16))
    for p in range(k // 512):
        a[p, :8] = np.random.permutation(np.resize(levels, 8))
        for g in range(8):
            far = levels[np.abs(levels - a[p, g]) >= 10]
            a[p, g + 8] = far[np.random.randint(len(far))]
    return np.exp2(a.ravel()).repeat(32)


BF16 = ml_dtypes.bfloat16


def bf(x):
    return np.asarray(x, np.float32).astype(BF16)


def f64(x):
    return np.asarray(x).astype(np.float64)


E2M1 = np.array([0.0, 0.5, 1.0, 1.5, 2.0, 3.0, 4.0, 6.0, -0.0, -0.5, -1.0, -1.5, -2.0, -3.0, -4.0, -6.0])


def pack_weight(w, fmt):
    k, n = w.shape
    w = f64(bf(w)).reshape(k // 32, 32, n)
    amax = np.abs(w).max(1)
    if fmt == "e4m3":
        byte = np.frexp(amax)[1] - 1 + 127 - 7
    else:
        mant, ex = np.frexp(amax / 6.0)
        byte = np.where(mant > 0.5, ex, ex - 1) + 127
    byte = np.clip(np.where(amax > 0, byte, 1), 1, 254)
    scaled = (w * np.exp2(127.0 - byte)[:, None, :]).reshape(k, n).astype(np.float32)
    by_word = np.ascontiguousarray(scaled.reshape(k // 512, 128, 4, n).transpose(0, 1, 3, 2))
    if fmt == "e4m3":
        words = by_word.astype(ml_dtypes.float8_e4m3fn).view(np.uint8)
    else:
        c = by_word.astype(ml_dtypes.float4_e2m1fn).view(np.uint8) & 0xF
        words = c[..., 0::2] | (c[..., 1::2] << 4)
    return np.ascontiguousarray(words), np.ascontiguousarray(byte.astype(np.uint8).reshape(k // 512, 16, n))


def unpack_weight(words, scales, fmt):
    g, p, n, _ = words.shape
    if fmt == "e4m3":
        vals = np.ascontiguousarray(words).view(ml_dtypes.float8_e4m3fn).astype(np.float64)
    else:
        nib = np.empty((g, p, n, 4), np.uint8)
        nib[..., 0::2] = words & 0xF
        nib[..., 1::2] = words >> 4
        vals = E2M1[nib]
    vals = vals * np.repeat(np.exp2(scales.astype(np.float64) - 127.0), 8, axis=1)[..., None]
    return vals.transpose(0, 1, 3, 2).reshape(g * 512, n)
def pack4(w):
    words, scales = pack_weight(w, "e2m1")
    return words.reshape(words.shape[0], 128, -1), scales


def unpack4(words, scales):
    return unpack_weight(words.reshape(words.shape[0], 128, -1, 2), scales, "e2m1")


M, D, F, N = 512, 2048, 1024, 4096


def sigmoid(a):
    return 1.0 / (1.0 + np.exp(-a))


def setup_inputs():
    s, t = mx_kscale(D), mx_kscale(F)
    x_words, x_scales = pack4(np.random.standard_normal((D, M)) * s[:, None])
    w_words, w_scales = pack4(np.random.standard_normal((D, F)) / np.sqrt(D) / s[:, None] * t)
    r_words, r_scales = pack4(np.random.standard_normal((D, F)) / np.sqrt(D) / s[:, None])
    v_words, v_scales = pack4(np.random.standard_normal((F, N)) / np.sqrt(F) / t[:, None])
    return {"x_words": x_words, "x_scales": x_scales,
            "w_words": w_words, "w_scales": w_scales,
            "r_words": r_words, "r_scales": r_scales,
            "v_words": v_words, "v_scales": v_scales,
            "u": bf(np.random.standard_normal((M, F)) * t),
            "b": bf(0.3 * np.random.standard_normal(F) * t),
            "rb": bf(0.5 * np.random.standard_normal(F)),
            "evidence": bf(np.exp(0.7 * np.random.standard_normal(M))),
            "user_bias": bf(0.5 * np.random.standard_normal(M)),
            "item_bias": bf(0.5 * np.random.standard_normal(N))}


def reference(x_words, x_scales, w_words, w_scales, r_words, r_scales, v_words, v_scales,
              u, b, rb, evidence, user_bias, item_bias):
    x = unpack4(x_words, x_scales).T
    w = unpack4(w_words, w_scales)
    r = unpack4(r_words, r_scales)
    v = unpack4(v_words, v_scales)
    prior = (x @ w) + f64(b)
    logit = (x @ r) + f64(rb) - np.log(f64(evidence))[:, None]
    trust = sigmoid(logit)
    z = trust * prior + (1.0 - trust) * f64(u)
    score = mxq(z, 1, "e4m3") @ v
    return score + f64(user_bias)[:, None] + f64(item_bias)[None, :]

@@ -1,0 +1,321 @@
+from contextlib import ExitStack
+
+import concourse.mybir as mybir
+from concourse.masks import make_identity
+
+F32 = mybir.dt.float32
+BF16 = mybir.dt.bfloat16
+U32 = mybir.dt.uint32
+I32 = mybir.dt.int32
+U8 = mybir.dt.uint8
+E2M1 = mybir.dt.float4_e2m1fn_x4
+E4M3 = mybir.dt.float8_e4m3fn_x4
+ALU = mybir.AluOpType
+ACT = mybir.ActivationFunctionType
+
+USERS, ATTRS, FACTORS, ITEMS = 512, 2048, 1024, 4096
+FLOPS = 2 * USERS * ATTRS * FACTORS * 2 + 2 * USERS * FACTORS * ITEMS
+
+P = 128
+COLS = 512
+KG = ATTRS // 512
+TILES = USERS // P
+HALVES = FACTORS // COLS
+UNITS = ITEMS // COLS
+
+VIA_SCALAR = (2, 6)
+
+
+def tile_gated_side_factorisation_f2_kernel(
+    tc, x_words, x_scales, w_words, w_scales, r_words, r_scales, v_words, v_scales,
+    u, b, rb, evidence, user_bias, item_bias, out,
+):
+    nc = tc.nc
+    with ExitStack() as ctx:
+        keep = ctx.enter_context(tc.tile_pool(name="keep", bufs=1))
+        work = ctx.enter_context(tc.tile_pool(name="work", bufs=3))
+        outs = ctx.enter_context(tc.tile_pool(name="outs", bufs=8))
+        psum = ctx.enter_context(tc.psum_pool(name="psum", bufs=8))
+        ctx.enter_context(tc.manual_schedule())
+
+        x_sb = keep.tile([P, KG, 2 * USERS], U8, name="x_sb", align_bytes=64)
+        w_sb = keep.tile([P, KG, 2 * FACTORS], U8, name="w_sb", align_bytes=64)
+        r_sb = keep.tile([P, KG, 2 * FACTORS], U8, name="r_sb", align_bytes=64)
+        v_sb = keep.tile([P, HALVES, 2 * ITEMS], U8, name="v_sb", align_bytes=64)
+        xs = keep.tile([P, KG, USERS], U8, name="xs", align_bytes=64)
+        ws = keep.tile([P, KG, FACTORS], U8, name="ws", align_bytes=64)
+        rs = keep.tile([P, KG, FACTORS], U8, name="rs", align_bytes=64)
+        vs = keep.tile([P, HALVES, ITEMS], U8, name="vs", align_bytes=64)
+        u_sb = keep.tile([P, TILES, FACTORS], BF16, name="u_sb", align_bytes=64)
+        rows = keep.tile([P, COLS], BF16, name="rows", align_bytes=64)
+        ident_bf = keep.tile([P, P], BF16, name="ident_bf", align_bytes=64)
+        ident_f = keep.tile([P, P], F32, name="ident_f", align_bytes=64)
+        b_bc = keep.tile([P, FACTORS], BF16, name="b_bc", align_bytes=64)
+        rb_bc = keep.tile([P, FACTORS], BF16, name="rb_bc", align_bytes=64)
+        ib_bc = keep.tile([P, ITEMS], BF16, name="ib_bc", align_bytes=64)
+        per_user = keep.tile([P, TILES, 8], F32, name="per_user", align_bytes=64)
+        log_ev = keep.tile([P, TILES], F32, name="log_ev", align_bytes=64)
+        warm = keep.tile([P, 8], F32, name="warm", align_bytes=64)
+        bu = keep.tile([P, TILES, FACTORS], F32, name="bu", align_bytes=64)
+        diff = keep.tile([P, TILES, FACTORS], F32, name="diff", align_bytes=64)
+        z_sb = keep.tile([P, TILES, FACTORS], BF16, name="z_sb", align_bytes=64)
+        zt = keep.tile([P, TILES, HALVES, COLS], BF16, name="zt", align_bytes=64)
+        zq = keep.tile([P, TILES, HALVES, P], U32, name="zq", align_bytes=64)
+        zs = keep.tile([P, TILES, HALVES, P], U8, name="zs", align_bytes=64)
+
+        def zero(tile_2d):
+            nc.vector.memset(tile_2d.bitcast(I32), 0)
+
+        def load_scales(queue, plane, scales, r):
+            queue.dma_start(
+                out=plane[r:P:32, :, :].bitcast(I32),
+                in_=scales.rearrange("g (q r) n -> r q g n", r=4)[r].bitcast(I32),
+            )
+
+        def load_words(tile, words, g0, g1, c0, c1):
+            nc.sync.dma_start(
+                out=tile[:, g0:g1, c0:c1],
+                in_=words[g0:g1, :, c0:c1].rearrange("g p c -> p g c"),
+            )
+
+        def load_u(m0, m1):
+            nc.sync.dma_start(
+                out=u_sb[:, m0:m1, :],
+                in_=u[m0 * P : m1 * P, :].rearrange("(m p) f -> p m f", p=P),
+            )
+
+        banks = {}
+
+        def bank(key):
+            tile = psum.tile([P, COLS], F32, name="bank")
+            banks[key] = tile
+            return tile
+
+        def first_pass(kind, m, h, g):
+            words, planes = (w_sb, ws) if kind == "w" else (r_sb, rs)
+            tile = bank((kind, m, h)) if g == 0 else banks[(kind, m, h)]
+            nc.tensor.matmul_mx(
+                out=tile[:],
+                lhsT=x_sb[:, g, 2 * P * m : 2 * P * (m + 1)].bitcast(E2M1),
+                lhsT_scale=xs[:, g, P * m : P * (m + 1)],
+                rhs=words[:, g, 2 * COLS * h : 2 * COLS * (h + 1)].bitcast(E2M1),
+                rhs_scale=planes[:, g, COLS * h : COLS * (h + 1)],
+                start=(g == 0),
+                stop=(g == KG - 1),
+            )
+
+        def first(kind, m, h):
+            for g in range(KG):
+                first_pass(kind, m, h, g)
+
+        def spread(row, dest, h):
+            tile = bank("spread")
+            nc.tensor.matmul(out=tile[:], lhsT=ident_bf[:, row : row + 1].to_broadcast([P, P]), rhs=rows[:],
+                             start=True, stop=True)
+            nc.scalar.copy(out=dest[:, COLS * h : COLS * (h + 1)], in_=tile[:])
+
+        def half(h):
+            return slice(COLS * h, COLS * (h + 1))
+
+        def step_bu(engine, m, h):
+            engine.tensor_tensor(out=bu[:, m, half(h)], in0=b_bc[:, half(h)], in1=u_sb[:, m, half(h)], op=ALU.subtract)
+
+        def step_diff(m, h):
+            nc.vector.tensor_tensor(out=diff[:, m, half(h)], in0=banks[("w", m, h)][:], in1=bu[:, m, half(h)], op=ALU.add)
+
+        trusts = {}
+
+        def step_logit(m, h):
+            trust = work.tile([P, COLS], F32, name="trust", align_bytes=64, bufs=6)
+            trusts[(m, h)] = trust
+            nc.vector.scalar_tensor_tensor(
+                out=trust[:], in0=banks[("r", m, h)][:], scalar=log_ev[:, m : m + 1], in1=rb_bc[:, half(h)],
+                op0=ALU.subtract, op1=ALU.add,
+            )
+            nc.scalar.activation(out=trust[:], in_=trust[:], func=ACT.Sigmoid)
+
+        def step_mul(engine, m, h):
+            engine.tensor_tensor(out=diff[:, m, half(h)], in0=trusts[(m, h)][:], in1=diff[:, m, half(h)], op=ALU.mult)
+
+        def step_z(engine, m, h):
+            engine.tensor_tensor(out=z_sb[:, m, half(h)], in0=diff[:, m, half(h)], in1=u_sb[:, m, half(h)], op=ALU.add)
+
+        def turn(m, h):
+            if h == 0:
+                bank(("t", m))
+            tile = banks[("t", m)]
+            words = z_sb[:, m, half(h)].bitcast(F32)
+            for e in range(2):
+                nc.tensor.transpose(tile[:, 256 * h + P * e : 256 * h + P * (e + 1)], words[:, e:256:2], ident_f[:])
+            nc.scalar.copy(
+                out=zt[:, m, h, :].bitcast(F32).rearrange("p (r e) -> p r e", e=2),
+                in_=tile[:, 256 * h : 256 * (h + 1)].rearrange("p (e r) -> p r e", e=2),
+            )
+
+        def quantise(m, h):
+            nc.vector.quantize_mx(out=zq[:, m, h, :].bitcast(E4M3), scales=zs[:, m, h, :], in_=zt[:, m, h, :])
+
+        staged = {}
+
+        def score(m, n):
+            tile = bank(("s", m, n))
+            for h in range(HALVES):
+                nc.tensor.matmul_mx(
+                    out=tile[:],
+                    lhsT=zq[:, m, h, :].bitcast(E4M3),
+                    lhsT_scale=zs[:, m, h, :],
+                    rhs=v_sb[:, h, 2 * COLS * n : 2 * COLS * (n + 1)].bitcast(E2M1),
+                    rhs_scale=vs[:, h, COLS * n : COLS * (n + 1)],
+                    start=(h == 0),
+                    stop=(h == HALVES - 1),
+                )
+
+        def leave(m, n):
+            if n % 2 == 0:
+                result = outs.tile([P, 2 * COLS], F32, name="result", align_bytes=64)
+                staged[m] = result
+            dest = staged[m][:, half(n % 2)]
+            if n in VIA_SCALAR:
+                part = work.tile([P, COLS], F32, name="part", align_bytes=64)
+                nc.scalar.activation(out=part[:], in_=banks[("s", m, n)][:], func=ACT.Identity, bias=per_user[:, m, 5:6])
+                nc.gpsimd.tensor_tensor(out=dest, in0=part[:], in1=ib_bc[:, half(n)], op=ALU.add)
+            else:
+                nc.vector.scalar_tensor_tensor(
+                    out=dest, in0=banks[("s", m, n)][:], scalar=per_user[:, m, 5:6], in1=ib_bc[:, half(n)],
+                    op0=ALU.add, op1=ALU.add,
+                )
+            last = m == TILES - 1 and n >= UNITS - 2
+            if last:
+                nc.sync.dma_start(out=out[P * m : P * (m + 1), COLS * n : COLS * (n + 1)], in_=dest)
+            elif n % 2 == 1:
+                nc.sync.dma_start(out=out[P * m : P * (m + 1), COLS * (n - 1) : COLS * (n + 1)], in_=staged[m][:])
+
+        V, G = nc.vector, nc.gpsimd
+
+        nc.vector.memset(xs[:].rearrange("p g n -> p (g n)").bitcast(I32), 0)
+        nc.vector.memset(ws[:].rearrange("p g n -> p (g n)").bitcast(I32), 0)
+        zero(rows[:])
+        nc.vector.memset(warm[:], 1.0)
+        nc.vector.memset(rs[:].rearrange("p g n -> p (g n)").bitcast(I32), 0)
+        nc.vector.memset(vs[:].rearrange("p g n -> p (g n)").bitcast(I32), 0)
+        load_words(x_sb, x_words, 0, 2, 0, 2 * USERS)
+        load_words(w_sb, w_words, 0, 1, 0, 2 * FACTORS)
+        for r in range(4):
+            load_scales(nc.scalar, xs, x_scales, r)
+        for r in range(2):
+            load_scales(nc.scalar, ws, w_scales, r)
+        nc.scalar.activation(out=warm[:, 0:4], in_=warm[:, 4:8], func=ACT.Ln)
+        for r in range(2, 4):
+            load_scales(nc.gpsimd, ws, w_scales, r)
+        nc.gpsimd.dma_start(out=rows[0:2, :], in_=b.rearrange("(c n) -> c n", n=COLS))
+        nc.gpsimd.dma_start(out=rows[2:4, :], in_=rb.rearrange("(c n) -> c n", n=COLS))
+        nc.gpsimd.dma_start(out=rows[4:5, :], in_=evidence.rearrange("(c n) -> c n", n=COLS))
+        nc.gpsimd.dma_start(out=rows[5:6, :], in_=user_bias.rearrange("(c n) -> c n", n=COLS))
+        make_identity(nc, ident_bf[:])
+        make_identity(nc, ident_f[:])
+        load_words(w_sb, w_words, 1, 2, 0, 2 * FACTORS)
+        load_words(x_sb, x_words, 2, 4, 0, 2 * USERS)
+        load_words(w_sb, w_words, 2, 4, 0, 2 * FACTORS)
+        load_u(0, 2)
+        load_u(2, 4)
+        for r in range(4):
+            load_scales(nc.sync, rs, r_scales, r)
+        load_words(r_sb, r_words, 0, 2, 0, 2 * FACTORS)
+        load_words(r_sb, r_words, 2, 4, 0, 2 * FACTORS)
+        for r in range(4):
+            load_scales(nc.sync, vs, v_scales, r)
+        for c in range(2):
+            load_words(v_sb, v_words, 0, 2, 2048 * c, 2048 * (c + 1))
+        nc.sync.dma_start(out=ib_bc[:], in_=item_bias.partition_broadcast(P))
+        for c in range(2, 4):
+            load_words(v_sb, v_words, 0, 2, 2048 * c, 2048 * (c + 1))
+
+        opening = [(m, h) for m in range(3) for h in range(HALVES)]
+        for g in range(KG):
+            if g == 2:
+                spread(0, b_bc, 0)
+                spread(1, b_bc, 1)
+            if g == 3:
+                small = bank("small")
+                for m in range(TILES):
+                    nc.tensor.matmul(out=small[:, 8 * m : 8 * (m + 1)], lhsT=rows[:, P * m : P * (m + 1)],
+                                     rhs=ident_bf[:, 0:8], start=True, stop=True)
+                nc.scalar.copy(out=per_user[:].rearrange("p m c -> p (m c)"), in_=small[:, 0:32])
+                nc.scalar.activation(out=log_ev[:], in_=per_user[:, :, 4], func=ACT.Ln)
+                nc.scalar.activation(out=warm[:, 0:4], in_=warm[:, 4:8], func=ACT.Sigmoid)
+                spread(2, rb_bc, 0)
+                spread(3, rb_bc, 1)
+            for m, h in opening:
+                first_pass("w", m, h, g)
+        for m in range(2):
+            for h in range(HALVES):
+                step_bu(V, m, h)
+                step_bu(G, m + 2, h)
+        for h in range(HALVES):
+            step_diff(0, h)
+        first("r", 0, 0)
+        step_logit(0, 0)
+        step_diff(1, 0)
+        first("r", 0, 1)
+        step_mul(G, 0, 0)
+        step_logit(0, 1)
+        step_z(G, 0, 0)
+        step_diff(1, 1)
+        first("r", 1, 0)
+        step_mul(V, 0, 1)
+        step_logit(1, 0)
+        step_z(V, 0, 1)
+        step_mul(G, 1, 0)
+        step_diff(2, 0)
+        first("r", 1, 1)
+        step_logit(1, 1)
+        step_z(G, 1, 0)
+        step_diff(2, 1)
+        first("w", 3, 0)
+        turn(0, 0)
+        turn(0, 1)
+        step_mul(V, 1, 1)
+        quantise(0, 0)
+        quantise(0, 1)
+        step_z(V, 1, 1)
+        first("w", 3, 1)
+        step_diff(3, 0)
+        step_diff(3, 1)
+        for n in range(4):
+            score(0, n)
+            leave(0, n)
+        turn(1, 0)
+        turn(1, 1)
+        quantise(1, 0)
+        quantise(1, 1)
+        for i in range(4):
+            m, h = divmod(i, 2)
+            first("r", 2 + m, h)
+            step_logit(2 + m, h)
+            score(0, 4 + i)
+            leave(0, 4 + i)
+            step_mul(V if i == 3 else G, 2 + m, h)
+            if i == 3:
+                turn(2, 0)
+                turn(2, 1)
+            score(1, 2 * i)
+            leave(1, 2 * i)
+            if i == 3:
+                quantise(2, 0)
+                quantise(2, 1)
+            step_z(V if i == 3 else G, 2 + m, h)
+            score(1, 2 * i + 1)
+            leave(1, 2 * i + 1)
+        for n in range(4):
+            score(2, n)
+            leave(2, n)
+        turn(3, 0)
+        turn(3, 1)
+        quantise(3, 0)
+        quantise(3, 1)
+        for n in range(4, UNITS):
+            score(2, n)
+            leave(2, n)
+        for n in range(UNITS):
+            score(3, n)
+            leave(3, n)

@@ -23,7 +23,7 @@ TILES = USERS // P
 HALVES = FACTORS // COLS
 UNITS = ITEMS // COLS
 
-VIA_SCALAR = (2, 6)
+VIA_SCALAR = (1, 4)
 
 
 def tile_gated_side_factorisation_f2_kernel(
@@ -48,6 +48,8 @@ def tile_gated_side_factorisation_f2_kernel(
         vs = keep.tile([P, HALVES, ITEMS], U8, name="vs", align_bytes=64)
         u_sb = keep.tile([P, TILES, FACTORS], BF16, name="u_sb", align_bytes=64)
         rows = keep.tile([P, COLS], BF16, name="rows", align_bytes=64)
+        rows_b = keep.tile([P, COLS], BF16, name="rows_b", align_bytes=64)
+        zeros = keep.tile([P, COLS], BF16, name="zeros", align_bytes=64)
         ident_bf = keep.tile([P, P], BF16, name="ident_bf", align_bytes=64)
         ident_f = keep.tile([P, P], F32, name="ident_f", align_bytes=64)
         b_bc = keep.tile([P, FACTORS], BF16, name="b_bc", align_bytes=64)
@@ -108,11 +110,11 @@ def tile_gated_side_factorisation_f2_kernel(
             for g in range(KG):
                 first_pass(kind, m, h, g)
 
-        def spread(row, dest, h):
+        def spread(src, row, dest, h, copy):
             tile = bank("spread")
-            nc.tensor.matmul(out=tile[:], lhsT=ident_bf[:, row : row + 1].to_broadcast([P, P]), rhs=rows[:],
+            nc.tensor.matmul(out=tile[:], lhsT=ident_bf[:, row : row + 1].to_broadcast([P, P]), rhs=src[:],
                              start=True, stop=True)
-            nc.scalar.copy(out=dest[:, COLS * h : COLS * (h + 1)], in_=tile[:])
+            copy(out=dest[:, COLS * h : COLS * (h + 1)], in_=tile[:])
 
         def half(h):
             return slice(COLS * h, COLS * (h + 1))
@@ -177,11 +179,11 @@ def tile_gated_side_factorisation_f2_kernel(
             dest = staged[m][:, half(n % 2)]
             if n in VIA_SCALAR:
                 part = work.tile([P, COLS], F32, name="part", align_bytes=64)
-                nc.scalar.activation(out=part[:], in_=banks[("s", m, n)][:], func=ACT.Identity, bias=per_user[:, m, 5:6])
+                nc.scalar.activation(out=part[:], in_=banks[("s", m, n)][:], func=ACT.Identity, bias=per_user[:, m, 1:2])
                 nc.gpsimd.tensor_tensor(out=dest, in0=part[:], in1=ib_bc[:, half(n)], op=ALU.add)
             else:
                 nc.vector.scalar_tensor_tensor(
-                    out=dest, in0=banks[("s", m, n)][:], scalar=per_user[:, m, 5:6], in1=ib_bc[:, half(n)],
+                    out=dest, in0=banks[("s", m, n)][:], scalar=per_user[:, m, 1:2], in1=ib_bc[:, half(n)],
                     op0=ALU.add, op1=ALU.add,
                 )
             last = m == TILES - 1 and n >= UNITS - 2
@@ -192,30 +194,30 @@ def tile_gated_side_factorisation_f2_kernel(
 
         V, G = nc.vector, nc.gpsimd
 
+        make_identity(nc, ident_bf[:])
+        make_identity(nc, ident_f[:])
+        zero(zeros[:])
+        zero(rows_b[:])
+        zero(rows[:])
         nc.vector.memset(xs[:].rearrange("p g n -> p (g n)").bitcast(I32), 0)
         nc.vector.memset(ws[:].rearrange("p g n -> p (g n)").bitcast(I32), 0)
-        zero(rows[:])
         nc.vector.memset(warm[:], 1.0)
         nc.vector.memset(rs[:].rearrange("p g n -> p (g n)").bitcast(I32), 0)
         nc.vector.memset(vs[:].rearrange("p g n -> p (g n)").bitcast(I32), 0)
+        nc.scalar.dma_start(out=rows_b[0:2, :], in_=b.rearrange("(c n) -> c n", n=COLS))
+        nc.scalar.dma_start(out=rows_b[2:4, :], in_=rb.rearrange("(c n) -> c n", n=COLS))
+        nc.scalar.activation(out=warm[:, 0:4], in_=warm[:, 4:8], func=ACT.Ln)
         load_words(x_sb, x_words, 0, 2, 0, 2 * USERS)
         load_words(w_sb, w_words, 0, 1, 0, 2 * FACTORS)
         for r in range(4):
-            load_scales(nc.scalar, xs, x_scales, r)
-        for r in range(2):
-            load_scales(nc.scalar, ws, w_scales, r)
-        nc.scalar.activation(out=warm[:, 0:4], in_=warm[:, 4:8], func=ACT.Ln)
-        for r in range(2, 4):
-            load_scales(nc.gpsimd, ws, w_scales, r)
-        nc.gpsimd.dma_start(out=rows[0:2, :], in_=b.rearrange("(c n) -> c n", n=COLS))
-        nc.gpsimd.dma_start(out=rows[2:4, :], in_=rb.rearrange("(c n) -> c n", n=COLS))
-        nc.gpsimd.dma_start(out=rows[4:5, :], in_=evidence.rearrange("(c n) -> c n", n=COLS))
-        nc.gpsimd.dma_start(out=rows[5:6, :], in_=user_bias.rearrange("(c n) -> c n", n=COLS))
-        make_identity(nc, ident_bf[:])
-        make_identity(nc, ident_f[:])
+            load_scales(nc.sync, xs, x_scales, r)
+        for r in range(4):
+            load_scales(nc.sync, ws, w_scales, r)
         load_words(w_sb, w_words, 1, 2, 0, 2 * FACTORS)
         load_words(x_sb, x_words, 2, 4, 0, 2 * USERS)
         load_words(w_sb, w_words, 2, 4, 0, 2 * FACTORS)
+        nc.sync.dma_start(out=rows[0:1, :], in_=evidence.rearrange("(c n) -> c n", n=COLS))
+        nc.sync.dma_start(out=rows[1:2, :], in_=user_bias.rearrange("(c n) -> c n", n=COLS))
         load_u(0, 2)
         load_u(2, 4)
         for r in range(4):
@@ -230,29 +232,37 @@ def tile_gated_side_factorisation_f2_kernel(
         for c in range(2, 4):
             load_words(v_sb, v_words, 0, 2, 2048 * c, 2048 * (c + 1))
 
+        def idle_pass():
+            tile = bank("idle")
+            nc.tensor.matmul(out=tile[:], lhsT=zeros[:, 0:P], rhs=zeros[:], start=True, stop=True)
+
+        for i in range(5):
+            idle_pass()
+        spread(rows_b, 0, b_bc, 0, nc.scalar.copy)
+        spread(rows_b, 1, b_bc, 1, nc.vector.tensor_copy)
+        spread(rows_b, 2, rb_bc, 0, nc.scalar.copy)
+        spread(rows_b, 3, rb_bc, 1, nc.vector.tensor_copy)
+        for i in range(3):
+            idle_pass()
+
         opening = [(m, h) for m in range(3) for h in range(HALVES)]
         for g in range(KG):
-            if g == 2:
-                spread(0, b_bc, 0)
-                spread(1, b_bc, 1)
             if g == 3:
                 small = bank("small")
                 for m in range(TILES):
                     nc.tensor.matmul(out=small[:, 8 * m : 8 * (m + 1)], lhsT=rows[:, P * m : P * (m + 1)],
                                      rhs=ident_bf[:, 0:8], start=True, stop=True)
                 nc.scalar.copy(out=per_user[:].rearrange("p m c -> p (m c)"), in_=small[:, 0:32])
-                nc.scalar.activation(out=log_ev[:], in_=per_user[:, :, 4], func=ACT.Ln)
+                nc.scalar.activation(out=log_ev[:], in_=per_user[:, :, 0], func=ACT.Ln)
                 nc.scalar.activation(out=warm[:, 0:4], in_=warm[:, 4:8], func=ACT.Sigmoid)
-                spread(2, rb_bc, 0)
-                spread(3, rb_bc, 1)
             for m, h in opening:
                 first_pass("w", m, h, g)
         for m in range(2):
             for h in range(HALVES):
                 step_bu(V, m, h)
                 step_bu(G, m + 2, h)
-        for h in range(HALVES):
-            step_diff(0, h)
+        step_diff(0, 0)
+        step_diff(0, 1)
         first("r", 0, 0)
         step_logit(0, 0)
         step_diff(1, 0)
@@ -263,57 +273,74 @@ def tile_gated_side_factorisation_f2_kernel(
         step_diff(1, 1)
         first("r", 1, 0)
         step_mul(V, 0, 1)
-        step_logit(1, 0)
-        step_z(V, 0, 1)
-        step_mul(G, 1, 0)
         step_diff(2, 0)
+        step_z(V, 0, 1)
+        step_logit(1, 0)
+        step_mul(G, 1, 0)
         first("r", 1, 1)
-        step_logit(1, 1)
-        step_z(G, 1, 0)
         step_diff(2, 1)
+        step_z(G, 1, 0)
+        step_logit(1, 1)
         first("w", 3, 0)
+        step_mul(G, 1, 1)
+        first("w", 3, 1)
         turn(0, 0)
         turn(0, 1)
-        step_mul(V, 1, 1)
+        step_diff(3, 0)
         quantise(0, 0)
         quantise(0, 1)
-        step_z(V, 1, 1)
-        first("w", 3, 1)
-        step_diff(3, 0)
         step_diff(3, 1)
+        step_z(G, 1, 1)
+        first("r", 2, 0)
+        step_logit(2, 0)
         for n in range(4):
             score(0, n)
             leave(0, n)
+        step_mul(G, 2, 0)
         turn(1, 0)
         turn(1, 1)
+        first("r", 2, 1)
         quantise(1, 0)
         quantise(1, 1)
-        for i in range(4):
-            m, h = divmod(i, 2)
-            first("r", 2 + m, h)
-            step_logit(2 + m, h)
-            score(0, 4 + i)
-            leave(0, 4 + i)
-            step_mul(V if i == 3 else G, 2 + m, h)
-            if i == 3:
-                turn(2, 0)
-                turn(2, 1)
-            score(1, 2 * i)
-            leave(1, 2 * i)
-            if i == 3:
-                quantise(2, 0)
-                quantise(2, 1)
-            step_z(V if i == 3 else G, 2 + m, h)
-            score(1, 2 * i + 1)
-            leave(1, 2 * i + 1)
+        step_logit(2, 1)
+        step_z(G, 2, 0)
+        step_mul(G, 2, 1)
+        for n in range(4, 8):
+            score(0, n)
+            leave(0, n)
+        step_z(G, 2, 1)
+        first("r", 3, 0)
+        step_logit(3, 0)
+        for n in range(4):
+            score(1, n)
+            leave(1, n)
+        step_mul(G, 3, 0)
+        first("r", 3, 1)
+        step_logit(3, 1)
+        turn(2, 0)
+        turn(2, 1)
+        step_z(G, 3, 0)
+        score(1, 4)
+        leave(1, 4)
+        step_mul(V, 3, 1)
+        quantise(2, 0)
+        quantise(2, 1)
+        score(1, 5)
+        leave(1, 5)
+        step_z(V, 3, 1)
+        for n in range(6, 8):
+            score(1, n)
+            leave(1, n)
         for n in range(4):
             score(2, n)
             leave(2, n)
         turn(3, 0)
         turn(3, 1)
+        score(2, 4)
+        leave(2, 4)
         quantise(3, 0)
         quantise(3, 1)
-        for n in range(4, UNITS):
+        for n in range(5, UNITS):
             score(2, n)
             leave(2, n)
         for n in range(UNITS):

@@ -23,8 +23,6 @@ TILES = USERS // P
 HALVES = FACTORS // COLS
 UNITS = ITEMS // COLS
 
-VIA_SCALAR = (1, 4)
-
 
 def tile_gated_side_factorisation_f2_kernel(
     tc, x_words, x_scales, w_words, w_scales, r_words, r_scales, v_words, v_scales,
@@ -61,7 +59,7 @@ def tile_gated_side_factorisation_f2_kernel(
         bu = keep.tile([P, TILES, FACTORS], F32, name="bu", align_bytes=64)
         diff = keep.tile([P, TILES, FACTORS], F32, name="diff", align_bytes=64)
         z_sb = keep.tile([P, TILES, FACTORS], BF16, name="z_sb", align_bytes=64)
-        zt = keep.tile([P, TILES, HALVES, COLS], BF16, name="zt", align_bytes=64)
+        zt = keep.tile([P, TILES, FACTORS], BF16, name="zt", align_bytes=64)
         zq = keep.tile([P, TILES, HALVES, P], U32, name="zq", align_bytes=64)
         zs = keep.tile([P, TILES, HALVES, P], U8, name="zs", align_bytes=64)
 
@@ -110,17 +108,18 @@ def tile_gated_side_factorisation_f2_kernel(
             for g in range(KG):
                 first_pass(kind, m, h, g)
 
-        def spread(src, row, dest, h, copy):
-            tile = bank("spread")
-            nc.tensor.matmul(out=tile[:], lhsT=ident_bf[:, row : row + 1].to_broadcast([P, P]), rhs=src[:],
+        def spread(row, key):
+            nc.tensor.matmul(out=bank(key)[:], lhsT=ident_bf[:, row : row + 1].to_broadcast([P, P]), rhs=rows_b[:],
                              start=True, stop=True)
-            copy(out=dest[:, COLS * h : COLS * (h + 1)], in_=tile[:])
 
         def half(h):
             return slice(COLS * h, COLS * (h + 1))
 
-        def step_bu(engine, m, h):
-            engine.tensor_tensor(out=bu[:, m, half(h)], in0=b_bc[:, half(h)], in1=u_sb[:, m, half(h)], op=ALU.subtract)
+        def step_bu(m, h):
+            if m < 2:
+                nc.vector.tensor_tensor(out=bu[:, m, half(h)], in0=banks[("b", h)][:], in1=u_sb[:, m, half(h)], op=ALU.subtract)
+            else:
+                nc.gpsimd.tensor_tensor(out=bu[:, m, half(h)], in0=b_bc[:, half(h)], in1=u_sb[:, m, half(h)], op=ALU.subtract)
 
         def step_diff(m, h):
             nc.vector.tensor_tensor(out=diff[:, m, half(h)], in0=banks[("w", m, h)][:], in1=bu[:, m, half(h)], op=ALU.add)
@@ -136,26 +135,30 @@ def tile_gated_side_factorisation_f2_kernel(
             )
             nc.scalar.activation(out=trust[:], in_=trust[:], func=ACT.Sigmoid)
 
-        def step_mul(engine, m, h):
-            engine.tensor_tensor(out=diff[:, m, half(h)], in0=trusts[(m, h)][:], in1=diff[:, m, half(h)], op=ALU.mult)
+        def step_mul(m, h):
+            nc.gpsimd.tensor_tensor(out=diff[:, m, half(h)], in0=trusts[(m, h)][:], in1=diff[:, m, half(h)], op=ALU.mult)
 
-        def step_z(engine, m, h):
-            engine.tensor_tensor(out=z_sb[:, m, half(h)], in0=diff[:, m, half(h)], in1=u_sb[:, m, half(h)], op=ALU.add)
+        def step_z(m, h):
+            nc.gpsimd.tensor_tensor(out=z_sb[:, m, half(h)], in0=diff[:, m, half(h)], in1=u_sb[:, m, half(h)], op=ALU.add)
 
-        def turn(m, h):
-            if h == 0:
-                bank(("t", m))
-            tile = banks[("t", m)]
-            words = z_sb[:, m, half(h)].bitcast(F32)
-            for e in range(2):
-                nc.tensor.transpose(tile[:, 256 * h + P * e : 256 * h + P * (e + 1)], words[:, e:256:2], ident_f[:])
+        def turn(m):
+            tile = bank(("t", m))
+            words = z_sb[:, m, :].bitcast(F32)
+            for h in range(HALVES):
+                for e in range(2):
+                    nc.tensor.transpose(tile[:, 256 * h + P * e : 256 * h + P * (e + 1)],
+                                        words[:, 256 * h + e : 256 * (h + 1) : 2], ident_f[:])
             nc.scalar.copy(
-                out=zt[:, m, h, :].bitcast(F32).rearrange("p (r e) -> p r e", e=2),
-                in_=tile[:, 256 * h : 256 * (h + 1)].rearrange("p (e r) -> p r e", e=2),
+                out=zt[:, m, :].bitcast(F32).rearrange("p (h r e) -> p h r e", h=HALVES, e=2),
+                in_=tile[:].rearrange("p (h e r) -> p h r e", h=HALVES, e=2),
             )
 
-        def quantise(m, h):
-            nc.vector.quantize_mx(out=zq[:, m, h, :].bitcast(E4M3), scales=zs[:, m, h, :], in_=zt[:, m, h, :])
+        def quantise(m):
+            nc.vector.quantize_mx(
+                out=zq[:, m, :, :].rearrange("p h r -> p (h r)").bitcast(E4M3),
+                scales=zs[:, m, :, :].rearrange("p h r -> p (h r)"),
+                in_=zt[:, m, :],
+            )
 
         staged = {}
 
@@ -177,22 +180,20 @@ def tile_gated_side_factorisation_f2_kernel(
                 result = outs.tile([P, 2 * COLS], F32, name="result", align_bytes=64)
                 staged[m] = result
             dest = staged[m][:, half(n % 2)]
-            if n in VIA_SCALAR:
-                part = work.tile([P, COLS], F32, name="part", align_bytes=64)
-                nc.scalar.activation(out=part[:], in_=banks[("s", m, n)][:], func=ACT.Identity, bias=per_user[:, m, 1:2])
-                nc.gpsimd.tensor_tensor(out=dest, in0=part[:], in1=ib_bc[:, half(n)], op=ALU.add)
-            else:
-                nc.vector.scalar_tensor_tensor(
-                    out=dest, in0=banks[("s", m, n)][:], scalar=per_user[:, m, 1:2], in1=ib_bc[:, half(n)],
-                    op0=ALU.add, op1=ALU.add,
-                )
+            nc.vector.scalar_tensor_tensor(
+                out=dest, in0=banks[("s", m, n)][:], scalar=per_user[:, m, 1:2], in1=ib_bc[:, half(n)],
+                op0=ALU.add, op1=ALU.add,
+            )
             last = m == TILES - 1 and n >= UNITS - 2
             if last:
                 nc.sync.dma_start(out=out[P * m : P * (m + 1), COLS * n : COLS * (n + 1)], in_=dest)
             elif n % 2 == 1:
                 nc.sync.dma_start(out=out[P * m : P * (m + 1), COLS * (n - 1) : COLS * (n + 1)], in_=staged[m][:])
 
-        V, G = nc.vector, nc.gpsimd
+        def scores(m, n0, n1):
+            for n in range(n0, n1):
+                score(m, n)
+                leave(m, n)
 
         make_identity(nc, ident_bf[:])
         make_identity(nc, ident_f[:])
@@ -233,15 +234,17 @@ def tile_gated_side_factorisation_f2_kernel(
             load_words(v_sb, v_words, 0, 2, 2048 * c, 2048 * (c + 1))
 
         def idle_pass():
-            tile = bank("idle")
-            nc.tensor.matmul(out=tile[:], lhsT=zeros[:, 0:P], rhs=zeros[:], start=True, stop=True)
+            nc.tensor.matmul(out=idle_bank[:], lhsT=zeros[:, 0:P], rhs=zeros[:], start=True, stop=True)
 
+        idle_bank = bank("idle")
         for i in range(5):
             idle_pass()
-        spread(rows_b, 0, b_bc, 0, nc.scalar.copy)
-        spread(rows_b, 1, b_bc, 1, nc.vector.tensor_copy)
-        spread(rows_b, 2, rb_bc, 0, nc.scalar.copy)
-        spread(rows_b, 3, rb_bc, 1, nc.vector.tensor_copy)
+        for h in range(HALVES):
+            spread(2 + h, ("rb", h))
+            nc.scalar.copy(out=rb_bc[:, half(h)], in_=banks[("rb", h)][:])
+        for h in range(HALVES):
+            spread(h, ("b", h))
+            nc.scalar.copy(out=b_bc[:, half(h)], in_=banks[("b", h)][:])
         for i in range(3):
             idle_pass()
 
@@ -257,92 +260,66 @@ def tile_gated_side_factorisation_f2_kernel(
                 nc.scalar.activation(out=warm[:, 0:4], in_=warm[:, 4:8], func=ACT.Sigmoid)
             for m, h in opening:
                 first_pass("w", m, h, g)
-        for m in range(2):
+        for m in range(TILES):
             for h in range(HALVES):
-                step_bu(V, m, h)
-                step_bu(G, m + 2, h)
+                step_bu(m, h)
         step_diff(0, 0)
         step_diff(0, 1)
         first("r", 0, 0)
         step_logit(0, 0)
         step_diff(1, 0)
         first("r", 0, 1)
-        step_mul(G, 0, 0)
+        step_mul(0, 0)
         step_logit(0, 1)
-        step_z(G, 0, 0)
+        step_z(0, 0)
         step_diff(1, 1)
         first("r", 1, 0)
-        step_mul(V, 0, 1)
+        step_mul(0, 1)
         step_diff(2, 0)
-        step_z(V, 0, 1)
+        step_z(0, 1)
         step_logit(1, 0)
-        step_mul(G, 1, 0)
         first("r", 1, 1)
+        step_mul(1, 0)
         step_diff(2, 1)
-        step_z(G, 1, 0)
+        step_z(1, 0)
         step_logit(1, 1)
         first("w", 3, 0)
-        step_mul(G, 1, 1)
-        first("w", 3, 1)
-        turn(0, 0)
-        turn(0, 1)
+        step_mul(1, 1)
         step_diff(3, 0)
-        quantise(0, 0)
-        quantise(0, 1)
+        first("w", 3, 1)
+        step_z(1, 1)
         step_diff(3, 1)
-        step_z(G, 1, 1)
         first("r", 2, 0)
         step_logit(2, 0)
-        for n in range(4):
-            score(0, n)
-            leave(0, n)
-        step_mul(G, 2, 0)
-        turn(1, 0)
-        turn(1, 1)
         first("r", 2, 1)
-        quantise(1, 0)
-        quantise(1, 1)
+        turn(0)
         step_logit(2, 1)
-        step_z(G, 2, 0)
-        step_mul(G, 2, 1)
-        for n in range(4, 8):
-            score(0, n)
-            leave(0, n)
-        step_z(G, 2, 1)
+        step_mul(2, 0)
+        quantise(0)
+        step_z(2, 0)
+        step_mul(2, 1)
         first("r", 3, 0)
         step_logit(3, 0)
-        for n in range(4):
-            score(1, n)
-            leave(1, n)
-        step_mul(G, 3, 0)
+        scores(0, 0, 4)
+        step_z(2, 1)
         first("r", 3, 1)
         step_logit(3, 1)
-        turn(2, 0)
-        turn(2, 1)
-        step_z(G, 3, 0)
-        score(1, 4)
-        leave(1, 4)
-        step_mul(V, 3, 1)
-        quantise(2, 0)
-        quantise(2, 1)
-        score(1, 5)
-        leave(1, 5)
-        step_z(V, 3, 1)
-        for n in range(6, 8):
-            score(1, n)
-            leave(1, n)
-        for n in range(4):
-            score(2, n)
-            leave(2, n)
-        turn(3, 0)
-        turn(3, 1)
-        score(2, 4)
-        leave(2, 4)
-        quantise(3, 0)
-        quantise(3, 1)
-        for n in range(5, UNITS):
-            score(2, n)
-            leave(2, n)
-        for n in range(UNITS):
-            score(3, n)
-            leave(3, n)
+        turn(1)
+        scores(0, 4, 6)
+        quantise(1)
+        step_mul(3, 0)
+        step_z(3, 0)
+        scores(0, 6, 8)
+        scores(1, 0, 3)
+        turn(2)
+        scores(1, 3, 4)
+        quantise(2)
+        step_mul(3, 1)
+        step_z(3, 1)
+        scores(1, 4, 8)
+        scores(2, 0, 3)
+        turn(3)
+        scores(2, 3, 4)
+        quantise(3)
+        scores(2, 4, 8)
+        scores(3, 0, 8)

from contextlib import ExitStack

import concourse.mybir as mybir
from concourse.masks import make_identity

F32 = mybir.dt.float32
BF16 = mybir.dt.bfloat16
U32 = mybir.dt.uint32
I32 = mybir.dt.int32
U8 = mybir.dt.uint8
E2M1 = mybir.dt.float4_e2m1fn_x4
E4M3 = mybir.dt.float8_e4m3fn_x4
ALU = mybir.AluOpType
ACT = mybir.ActivationFunctionType

USERS, ATTRS, FACTORS, ITEMS = 512, 2048, 1024, 4096
FLOPS = 2 * USERS * ATTRS * FACTORS * 2 + 2 * USERS * FACTORS * ITEMS

P = 128
COLS = 512
KG = ATTRS // 512
TILES = USERS // P
HALVES = FACTORS // COLS
UNITS = ITEMS // COLS


def tile_gated_side_factorisation_f2_kernel(
    tc, x_words, x_scales, w_words, w_scales, r_words, r_scales, v_words, v_scales,
    u, b, rb, evidence, user_bias, item_bias, out,
):
    nc = tc.nc
    with ExitStack() as ctx:
        keep = ctx.enter_context(tc.tile_pool(name="keep", bufs=1))
        work = ctx.enter_context(tc.tile_pool(name="work", bufs=3))
        outs = ctx.enter_context(tc.tile_pool(name="outs", bufs=8))
        psum = ctx.enter_context(tc.psum_pool(name="psum", bufs=8))
        ctx.enter_context(tc.manual_schedule())

        x_sb = keep.tile([P, KG, 2 * USERS], U8, name="x_sb", align_bytes=64)
        w_sb = keep.tile([P, KG, 2 * FACTORS], U8, name="w_sb", align_bytes=64)
        r_sb = keep.tile([P, KG, 2 * FACTORS], U8, name="r_sb", align_bytes=64)
        v_sb = keep.tile([P, HALVES, 2 * ITEMS], U8, name="v_sb", align_bytes=64)
        xs = keep.tile([P, KG, USERS], U8, name="xs", align_bytes=64)
        ws = keep.tile([P, KG, FACTORS], U8, name="ws", align_bytes=64)
        rs = keep.tile([P, KG, FACTORS], U8, name="rs", align_bytes=64)
        vs = keep.tile([P, HALVES, ITEMS], U8, name="vs", align_bytes=64)
        u_sb = keep.tile([P, TILES, FACTORS], BF16, name="u_sb", align_bytes=64)
        rows = keep.tile([P, COLS], BF16, name="rows", align_bytes=64)
        rows_b = keep.tile([P, COLS], BF16, name="rows_b", align_bytes=64)
        zeros = keep.tile([P, COLS], BF16, name="zeros", align_bytes=64)
        ident_bf = keep.tile([P, P], BF16, name="ident_bf", align_bytes=64)
        ident_f = keep.tile([P, P], F32, name="ident_f", align_bytes=64)
        b_bc = keep.tile([P, FACTORS], BF16, name="b_bc", align_bytes=64)
        rb_bc = keep.tile([P, FACTORS], BF16, name="rb_bc", align_bytes=64)
        ib_bc = keep.tile([P, ITEMS], BF16, name="ib_bc", align_bytes=64)
        per_user = keep.tile([P, TILES, 8], F32, name="per_user", align_bytes=64)
        log_ev = keep.tile([P, TILES], F32, name="log_ev", align_bytes=64)
        warm = keep.tile([P, 8], F32, name="warm", align_bytes=64)
        bu = keep.tile([P, TILES, FACTORS], F32, name="bu", align_bytes=64)
        diff = keep.tile([P, TILES, FACTORS], F32, name="diff", align_bytes=64)
        z_sb = keep.tile([P, TILES, FACTORS], BF16, name="z_sb", align_bytes=64)
        zt = keep.tile([P, TILES, FACTORS], BF16, name="zt", align_bytes=64)
        zq = keep.tile([P, TILES, HALVES, P], U32, name="zq", align_bytes=64)
        zs = keep.tile([P, TILES, HALVES, P], U8, name="zs", align_bytes=64)

        def zero(tile_2d):
            nc.vector.memset(tile_2d.bitcast(I32), 0)

        def load_scales(queue, plane, scales, r):
            queue.dma_start(
                out=plane[r:P:32, :, :].bitcast(I32),
                in_=scales.rearrange("g (q r) n -> r q g n", r=4)[r].bitcast(I32),
            )

        def load_words(tile, words, g0, g1, c0, c1):
            nc.sync.dma_start(
                out=tile[:, g0:g1, c0:c1],
                in_=words[g0:g1, :, c0:c1].rearrange("g p c -> p g c"),
            )

        def load_u(m0, m1):
            nc.sync.dma_start(
                out=u_sb[:, m0:m1, :],
                in_=u[m0 * P : m1 * P, :].rearrange("(m p) f -> p m f", p=P),
            )

        banks = {}

        def bank(key):
            tile = psum.tile([P, COLS], F32, name="bank")
            banks[key] = tile
            return tile

        def first_pass(kind, m, h, g):
            words, planes = (w_sb, ws) if kind == "w" else (r_sb, rs)
            tile = bank((kind, m, h)) if g == 0 else banks[(kind, m, h)]
            nc.tensor.matmul_mx(
                out=tile[:],
                lhsT=x_sb[:, g, 2 * P * m : 2 * P * (m + 1)].bitcast(E2M1),
                lhsT_scale=xs[:, g, P * m : P * (m + 1)],
                rhs=words[:, g, 2 * COLS * h : 2 * COLS * (h + 1)].bitcast(E2M1),
                rhs_scale=planes[:, g, COLS * h : COLS * (h + 1)],
                start=(g == 0),
                stop=(g == KG - 1),
            )

        def first(kind, m, h):
            for g in range(KG):
                first_pass(kind, m, h, g)

        def spread(row, key):
            nc.tensor.matmul(out=bank(key)[:], lhsT=ident_bf[:, row : row + 1].to_broadcast([P, P]), rhs=rows_b[:],
                             start=True, stop=True)

        def half(h):
            return slice(COLS * h, COLS * (h + 1))

        def step_bu(m, h):
            if m < 2:
                nc.vector.tensor_tensor(out=bu[:, m, half(h)], in0=banks[("b", h)][:], in1=u_sb[:, m, half(h)], op=ALU.subtract)
            else:
                nc.gpsimd.tensor_tensor(out=bu[:, m, half(h)], in0=b_bc[:, half(h)], in1=u_sb[:, m, half(h)], op=ALU.subtract)

        def step_diff(m, h):
            nc.vector.tensor_tensor(out=diff[:, m, half(h)], in0=banks[("w", m, h)][:], in1=bu[:, m, half(h)], op=ALU.add)

        trusts = {}

        def step_logit(m, h):
            trust = work.tile([P, COLS], F32, name="trust", align_bytes=64, bufs=6)
            trusts[(m, h)] = trust
            nc.vector.scalar_tensor_tensor(
                out=trust[:], in0=banks[("r", m, h)][:], scalar=log_ev[:, m : m + 1], in1=rb_bc[:, half(h)],
                op0=ALU.subtract, op1=ALU.add,
            )
            nc.scalar.activation(out=trust[:], in_=trust[:], func=ACT.Sigmoid)

        def step_mul(m, h):
            nc.gpsimd.tensor_tensor(out=diff[:, m, half(h)], in0=trusts[(m, h)][:], in1=diff[:, m, half(h)], op=ALU.mult)

        def step_z(m, h):
            nc.gpsimd.tensor_tensor(out=z_sb[:, m, half(h)], in0=diff[:, m, half(h)], in1=u_sb[:, m, half(h)], op=ALU.add)

        def turn(m):
            tile = bank(("t", m))
            words = z_sb[:, m, :].bitcast(F32)
            for h in range(HALVES):
                for e in range(2):
                    nc.tensor.transpose(tile[:, 256 * h + P * e : 256 * h + P * (e + 1)],
                                        words[:, 256 * h + e : 256 * (h + 1) : 2], ident_f[:])
            nc.scalar.copy(
                out=zt[:, m, :].bitcast(F32).rearrange("p (h r e) -> p h r e", h=HALVES, e=2),
                in_=tile[:].rearrange("p (h e r) -> p h r e", h=HALVES, e=2),
            )

        def quantise(m):
            nc.vector.quantize_mx(
                out=zq[:, m, :, :].rearrange("p h r -> p (h r)").bitcast(E4M3),
                scales=zs[:, m, :, :].rearrange("p h r -> p (h r)"),
                in_=zt[:, m, :],
            )

        staged = {}

        def score(m, n):
            tile = bank(("s", m, n))
            for h in range(HALVES):
                nc.tensor.matmul_mx(
                    out=tile[:],
                    lhsT=zq[:, m, h, :].bitcast(E4M3),
                    lhsT_scale=zs[:, m, h, :],
                    rhs=v_sb[:, h, 2 * COLS * n : 2 * COLS * (n + 1)].bitcast(E2M1),
                    rhs_scale=vs[:, h, COLS * n : COLS * (n + 1)],
                    start=(h == 0),
                    stop=(h == HALVES - 1),
                )

        def leave(m, n):
            if n % 2 == 0:
                result = outs.tile([P, 2 * COLS], F32, name="result", align_bytes=64)
                staged[m] = result
            dest = staged[m][:, half(n % 2)]
            nc.vector.scalar_tensor_tensor(
                out=dest, in0=banks[("s", m, n)][:], scalar=per_user[:, m, 1:2], in1=ib_bc[:, half(n)],
                op0=ALU.add, op1=ALU.add,
            )
            last = m == TILES - 1 and n >= UNITS - 2
            if last:
                nc.sync.dma_start(out=out[P * m : P * (m + 1), COLS * n : COLS * (n + 1)], in_=dest)
            elif n % 2 == 1:
                nc.sync.dma_start(out=out[P * m : P * (m + 1), COLS * (n - 1) : COLS * (n + 1)], in_=staged[m][:])

        def scores(m, n0, n1):
            for n in range(n0, n1):
                score(m, n)
                leave(m, n)

        make_identity(nc, ident_bf[:])
        make_identity(nc, ident_f[:])
        zero(zeros[:])
        zero(rows_b[:])
        zero(rows[:])
        nc.vector.memset(xs[:].rearrange("p g n -> p (g n)").bitcast(I32), 0)
        nc.vector.memset(ws[:].rearrange("p g n -> p (g n)").bitcast(I32), 0)
        nc.vector.memset(warm[:], 1.0)
        nc.vector.memset(rs[:].rearrange("p g n -> p (g n)").bitcast(I32), 0)
        nc.vector.memset(vs[:].rearrange("p g n -> p (g n)").bitcast(I32), 0)
        nc.scalar.dma_start(out=rows_b[0:2, :], in_=b.rearrange("(c n) -> c n", n=COLS))
        nc.scalar.dma_start(out=rows_b[2:4, :], in_=rb.rearrange("(c n) -> c n", n=COLS))
        nc.scalar.activation(out=warm[:, 0:4], in_=warm[:, 4:8], func=ACT.Ln)
        load_words(x_sb, x_words, 0, 2, 0, 2 * USERS)
        load_words(w_sb, w_words, 0, 1, 0, 2 * FACTORS)
        for r in range(4):
            load_scales(nc.sync, xs, x_scales, r)
        for r in range(4):
            load_scales(nc.sync, ws, w_scales, r)
        load_words(w_sb, w_words, 1, 2, 0, 2 * FACTORS)
        load_words(x_sb, x_words, 2, 4, 0, 2 * USERS)
        load_words(w_sb, w_words, 2, 4, 0, 2 * FACTORS)
        nc.sync.dma_start(out=rows[0:1, :], in_=evidence.rearrange("(c n) -> c n", n=COLS))
        nc.sync.dma_start(out=rows[1:2, :], in_=user_bias.rearrange("(c n) -> c n", n=COLS))
        load_u(0, 2)
        load_u(2, 4)
        for r in range(4):
            load_scales(nc.sync, rs, r_scales, r)
        load_words(r_sb, r_words, 0, 2, 0, 2 * FACTORS)
        load_words(r_sb, r_words, 2, 4, 0, 2 * FACTORS)
        for r in range(4):
            load_scales(nc.sync, vs, v_scales, r)
        for c in range(2):
            load_words(v_sb, v_words, 0, 2, 2048 * c, 2048 * (c + 1))
        nc.sync.dma_start(out=ib_bc[:], in_=item_bias.partition_broadcast(P))
        for c in range(2, 4):
            load_words(v_sb, v_words, 0, 2, 2048 * c, 2048 * (c + 1))

        def idle_pass():
            nc.tensor.matmul(out=idle_bank[:], lhsT=zeros[:, 0:P], rhs=zeros[:], start=True, stop=True)

        idle_bank = bank("idle")
        for i in range(5):
            idle_pass()
        for h in range(HALVES):
            spread(2 + h, ("rb", h))
            nc.scalar.copy(out=rb_bc[:, half(h)], in_=banks[("rb", h)][:])
        for h in range(HALVES):
            spread(h, ("b", h))
            nc.scalar.copy(out=b_bc[:, half(h)], in_=banks[("b", h)][:])
        for i in range(3):
            idle_pass()

        opening = [(m, h) for m in range(3) for h in range(HALVES)]
        for g in range(KG):
            if g == 3:
                small = bank("small")
                for m in range(TILES):
                    nc.tensor.matmul(out=small[:, 8 * m : 8 * (m + 1)], lhsT=rows[:, P * m : P * (m + 1)],
                                     rhs=ident_bf[:, 0:8], start=True, stop=True)
                nc.scalar.copy(out=per_user[:].rearrange("p m c -> p (m c)"), in_=small[:, 0:32])
                nc.scalar.activation(out=log_ev[:], in_=per_user[:, :, 0], func=ACT.Ln)
                nc.scalar.activation(out=warm[:, 0:4], in_=warm[:, 4:8], func=ACT.Sigmoid)
            for m, h in opening:
                first_pass("w", m, h, g)
        for m in range(TILES):
            for h in range(HALVES):
                step_bu(m, h)
        step_diff(0, 0)
        step_diff(0, 1)
        first("r", 0, 0)
        step_logit(0, 0)
        step_diff(1, 0)
        first("r", 0, 1)
        step_mul(0, 0)
        step_logit(0, 1)
        step_z(0, 0)
        step_diff(1, 1)
        first("r", 1, 0)
        step_mul(0, 1)
        step_diff(2, 0)
        step_z(0, 1)
        step_logit(1, 0)
        first("r", 1, 1)
        step_mul(1, 0)
        step_diff(2, 1)
        step_z(1, 0)
        step_logit(1, 1)
        first("w", 3, 0)
        step_mul(1, 1)
        step_diff(3, 0)
        first("w", 3, 1)
        step_z(1, 1)
        step_diff(3, 1)
        first("r", 2, 0)
        step_logit(2, 0)
        first("r", 2, 1)
        turn(0)
        step_logit(2, 1)
        step_mul(2, 0)
        quantise(0)
        step_z(2, 0)
        step_mul(2, 1)
        first("r", 3, 0)
        step_logit(3, 0)
        scores(0, 0, 4)
        step_z(2, 1)
        first("r", 3, 1)
        step_logit(3, 1)
        turn(1)
        scores(0, 4, 6)
        quantise(1)
        step_mul(3, 0)
        step_z(3, 0)
        scores(0, 6, 8)
        scores(1, 0, 3)
        turn(2)
        scores(1, 3, 4)
        quantise(2)
        step_mul(3, 1)
        step_z(3, 1)
        scores(1, 4, 8)
        scores(2, 0, 3)
        turn(3)
        scores(2, 3, 4)
        quantise(3)
        scores(2, 4, 8)
        scores(3, 0, 8)
